import numpy as np, ml_dtypes
CORES = [17,57,65,89,97,121]
N = 6
import mx_ref
NC, ROOT = 512, 4
BF = ml_dtypes.bfloat16
def cut(t, i, w=512):
    return t[:, w * i:w * i + w]
def term(a, B):
    return np.stack([np.maximum(mx_ref.matmul(mx_ref.quantize(cut(a, i)), B), 0) for i in range(4)], axis=2).reshape(128, -1)
def setup_inputs(rng):
    def f(*shape):
        return mx_ref.flush((rng.standard_normal(shape, dtype=np.float32) * np.exp2(rng.integers(-2, 3, shape[:-1] + (1,)))).astype(BF))
    return {"a": f(N, 128, 4 * 512), "b": f(N, 128, 4 * NC)}
def setup_inputs_blocks(rng):
    d = setup_inputs(rng)
    for k in ("a", "b"): d[k] = mx_ref.spread(d[k], rng, 2)
    return d
def setup_inputs_wide(rng):
    d = setup_inputs(rng)
    for k in ("a", "b"): d[k] = mx_ref.flush((d[k].astype(np.float32) * np.exp2(rng.integers(-4, 5, (N, 1, 1))).astype(np.float32)).astype(BF))
    return d
def setup_inputs_lossless(rng):
    a = np.zeros((N, 128, 4 * 128, 4), np.float32)
    for r in range(N):
        k = rng.integers(0, 512, size=4 * 128)
        a[r, k // 4, np.arange(4 * 128), k % 4] = 1.0
    size = np.repeat(2.0 ** rng.integers(-4, 5, size=(1, 1, (4 * NC) // 4)), 4, axis=2)
    b = (rng.random((N, 128, 4 * NC)) < 0.8) * size
    return {"a": a.reshape(N, 128, 4 * 512).astype(BF), "b": b.astype(np.float32).astype(BF)}
def reference(a, b):
    B0 = mx_ref.quantize(b[ROOT])
    T = [term(a[r], B0) for r in range(N)]
    y = np.zeros((N, 128, 4 * NC), np.float32)
    y[:] = mx_ref.total(T)
    return {"y": y}

@@ -1,0 +1,199 @@
+from concourse.bass import DstId, RemoteDMATransfer
+from concourse.mybir import dt, AluOpType, ActivationFunctionType as AF
+
+F8, U8 = "float8_e4m3fn_x4", "uint8"
+SCRATCH = {
+    "at": ("sbuf", [128, 2048], "bfloat16"),
+    "bt": ("sbuf", [128, 2048], "bfloat16"),
+    "sel": ("sbuf", [128, 2048], "bfloat16"),
+    "qac": ("sbuf", [128, 512], F8), "qap": ("sbuf", [128, 512], U8),
+    "qbc": ("sbuf", [128, 512], F8), "qbp": ("sbuf", [128, 512], U8),
+    "qsc": ("sbuf", [128, 512], F8), "qsp": ("sbuf", [128, 512], U8),
+    "rc": ("sbuf", [128, 512], F8), "rp": ("sbuf", [128, 512], U8),
+    "ysb": ("sbuf", [128, 2048], "float32"),
+    "ac": ("sbuf", [128, 768], F8), "ap": ("sbuf", [128, 768], U8),
+    "bc": ("sbuf", [128, 512], F8), "bp": ("sbuf", [128, 512], U8),
+    "relu": ("sbuf", [128, 1536], "float32"),
+    "acc": ("sbuf", [128, 1024], "float32"),
+    "tile": ("sbuf", [128, 512], "bfloat16"),
+    "qtc": ("sbuf", [128, 128], F8), "qtp": ("sbuf", [128, 128], U8),
+    "ps": ("psum", [128, 4096], "float32"),
+}
+SEMAPHORES = (["la0", "la1", "lb0", "lb1", "ones", "onehot", "qa", "qb0", "qb1", "qs", "sent", "res0", "res1",
+               "cv0", "cv1", "cs0", "cs1", "st0", "st1", "a", "x", "b", "bf", "pad", "qt"]
+              + ["mm%d" % k for k in range(8)] + ["re%d" % k for k in range(6)] + ["ad%d" % k for k in range(5)])
+NCORES = 128
+
+
+def _bits(mask):
+    return [1 << k for k in range(mask.bit_length()) if (mask >> k) & 1]
+
+
+def _split(mask, n):
+    e = _bits(mask)
+    m = len(e) // n
+    return [sum(e[k * m:(k + 1) * m]) for k in range(n)]
+
+
+def _dst(topo, c):
+    rid, pid, _ = topo.addr(c)
+    return DstId(rid=rid, pnc=pid)
+
+
+def _plan(T, topo):
+    root = T.cores[T.root]
+    home = topo.chip(root)
+    gates = [c for c in range(NCORES) if c not in T.cores and all(topo.may_write(c, r) for r in T.cores)]
+    near = [c for c in gates if topo.chip(c) == home][:4]
+    far = [c for c in gates if topo.mates(topo.chip(c), home)]
+    pair = []
+    for c in near:
+        m = [f for f in far if topo.die(f) == topo.die(c) and f not in pair]
+        pair.append(m[0])
+    g0 = [r for r in T.cores if topo.may_write(r, near[0])]
+    g1 = [r for r in T.cores if r not in g0]
+    return root, near, pair, g0, g1
+
+
+def rank_program(g, core, T, topo):
+    root, near, far, g0, g1 = _plan(T, topo)
+    sites = [near, far]
+    S = T.sem
+    sent = [0]
+
+    def codes(buf, a, b):
+        return buf[:, a:b].bitcast(dt.uint8)
+
+    def fused(parts):
+        g.remote_dma_fused([RemoteDMATransfer(dst_ids=[_dst(topo, d) for d in ds], dma_engine_mask=m, remote_sem=sem,
+                                              srcs=[src], dsts=[dst] * len(ds))
+                            for ds, m, src, dst, sem in parts], local_sem=S.sent)
+        sent[0] += sum(len(_bits(p[1])) for p in parts)
+
+    def a_masks(r):
+        to = near if r in g0 else far
+        return to, _split(topo.mask(r, to[0]), 4)
+
+    if core in T.cores:
+        to, masks = a_masks(core)
+        slot = (g0 + g1).index(core)
+        g.sync.dma_start(T.at[:, 0:1024], T.a[:, 0:1024]).then_inc(S.la0, 16)
+        g.scalar.dma_start(T.at[:, 1024:2048], T.a[:, 1024:2048]).then_inc(S.la1, 16)
+        if core == root:
+            g.sync.dma_start(T.bt[:, 1024:2048], T.b[:, 1024:2048]).then_inc(S.lb1, 16)
+            g.scalar.dma_start(T.bt[:, 0:1024], T.b[:, 0:1024]).then_inc(S.lb0, 16)
+        g.vector.memset(T.sel[:], 1.0).then_inc(S.ones, 1)
+        for k, s in enumerate((S.la0, S.la1)):
+            g.vector.wait_ge(s, 16)
+            g.vector.quantize_mx(T.qac[:, 256 * k:256 * k + 256], T.qap[:, 256 * k:256 * k + 256],
+                                 T.at[:, 1024 * k:1024 * k + 1024]).then_inc(S.qa, 1)
+        if core == root:
+            for k, s, q in ((1, S.lb1, S.qb1), (0, S.lb0, S.qb0)):
+                g.vector.wait_ge(s, 16)
+                g.vector.quantize_mx(T.qbc[:, 256 * k:256 * k + 256], T.qbp[:, 256 * k:256 * k + 256],
+                                     T.bt[:, 1024 * k:1024 * k + 1024]).then_inc(q, 1)
+        g.wait_ge(S.qa, 2)
+        o = 128 * slot
+        fused([([to[i]], masks[i], codes(T.qac, 128 * i, 128 * i + 128), codes(T.ac, o, o + 128), S.a) for i in range(4)])
+        fused([([to[i]], masks[i], T.qap[:, 128 * i:128 * i + 128], T.ap[:, o:o + 128], S.a) for i in range(4)])
+        if core == root:
+            m = topo.mask(core, near[0])
+            for k, q, s in ((1, S.qb1, S.bf), (0, S.qb0, S.b)):
+                g.wait_ge(q, 1)
+                fused([(near, m, codes(T.qbc, 256 * k, 256 * k + 256), codes(T.bc, 256 * k, 256 * k + 256), s)])
+                fused([(near, m, T.qbp[:, 256 * k:256 * k + 256], T.bp[:, 256 * k:256 * k + 256], s)])
+        g.wait_ge(S.ones, 1)
+        g.affine_select(T.sel[:], T.sel[:], [[1, 4], [-1, 512]], AluOpType.is_equal, 0.0, 0, 4).then_inc(S.onehot, 1)
+        g.vector.wait_ge(S.onehot, 1)
+        g.vector.quantize_mx(T.qsc[:], T.qsp[:], T.sel[:]).then_inc(S.qs, 1)
+        g.tensor.wait_ge(S.qs, 1)
+        for h in range(2):
+            need = 0
+            for c in sites[h]:
+                need += 2 * len(_bits(_result_mask(topo, c, core, root)))
+            g.tensor.wait_ge(S["res%d" % h], need)
+            for b in range(4):
+                k = 4 * h + b
+                g.tensor.matmul_mx(T.ps[:, 512 * k:512 * k + 256], T.qsc[:, 128 * b:128 * b + 128],
+                                   T.qsp[:, 128 * b:128 * b + 128], T.rc[:, 256 * h:256 * h + 256],
+                                   T.rp[:, 256 * h:256 * h + 256], True, True).then_inc(S["mm%d" % k], 1)
+        for h in range(2):
+            for b in range(4):
+                k = 4 * h + b
+                q = g.vector if b % 2 == 0 else g.scalar
+                q.wait_ge(S["mm%d" % k], 1)
+                for i in range(4):
+                    o = 1024 * h + 4 * b + i
+                    out = T.ysb[:, o:1024 * h + 1024:16]
+                    src = T.ps[:, 512 * k + 64 * i:512 * k + 64 * i + 64]
+                    if b % 2 == 0:
+                        g.vector.tensor_copy(out, src).then_inc(S["cv%d" % h], 1)
+                    else:
+                        g.scalar.activation(out, src, AF.Copy).then_inc(S["cs%d" % h], 1)
+            d = g.sync if h == 0 else g.scalar
+            d.wait_ge(S["cv%d" % h], 8)
+            d.wait_ge(S["cs%d" % h], 8)
+            d.dma_start(T.y[:, 1024 * h:1024 * h + 1024], T.ysb[:, 1024 * h:1024 * h + 1024]).then_inc(S["st%d" % h], 16)
+            d.wait_ge(S["st%d" % h], 16)
+        g.wait_ge(S.sent, sent[0])
+        return
+
+    if core not in near and core not in far:
+        return
+    h = 0 if core in near else 1
+    i = sites[h].index(core)
+    partner = sites[1 - h][i]
+    pm = topo.mask(core, partner)
+    own, other = (g0, g1) if h == 0 else (g1, g0)
+    n_a = sum(2 * len(_bits(a_masks(r)[1][i])) for r in own)
+    n_x = 2 * len(_bits(topo.mask(partner, core)))
+    n_b = 2 * len(_bits(topo.mask(root, core) if h == 0 else topo.mask(near[i], core)))
+    first = (0, 384) if h == 0 else (384, 768)
+    g.wait_ge(S.a, n_a)
+    fused([([partner], pm, codes(T.ac, *first), codes(T.ac, *first), S.x)])
+    fused([([partner], pm, T.ap[:, first[0]:first[1]], T.ap[:, first[0]:first[1]], S.x)])
+    if h == 0:
+        g.wait_ge(S.bf, n_b)
+        fused([([partner], pm, codes(T.bc, 256, 512), codes(T.bc, 256, 512), S.b)])
+        fused([([partner], pm, T.bp[:, 256:512], T.bp[:, 256:512], S.b)])
+    order = [(g0 + g1).index(r) for r in own + other]
+    g.tensor.wait_ge(S.b, n_b)
+    g.tensor.wait_ge(S.a, n_a)
+    for k, s in enumerate(order):
+        if k == len(own):
+            g.tensor.wait_ge(S.x, n_x)
+        g.tensor.matmul_mx(T.ps[:, 512 * k:512 * k + 256], T.ac[:, 128 * s:128 * s + 128], T.ap[:, 128 * s:128 * s + 128],
+                           T.bc[:, 256 * h:256 * h + 256], T.bp[:, 256 * h:256 * h + 256],
+                           True, True).then_inc(S["mm%d" % k], 1)
+    for k in range(6):
+        g.scalar.wait_ge(S["mm%d" % k], 1)
+        g.scalar.activation(T.relu[:, 256 * k:256 * k + 256], T.ps[:, 512 * k:512 * k + 256], AF.Relu).then_inc(S["re%d" % k], 1)
+    g.vector.memset(T.tile[:, 256:512], 0.0).then_inc(S.pad, 1)
+    g.vector.wait_ge(S.re0, 1)
+    for k in range(5):
+        a = T.relu[:, 0:256] if k == 0 else T.acc[:, 256 * k - 256:256 * k]
+        o = T.tile[:, 0:256] if k == 4 else T.acc[:, 256 * k:256 * k + 256]
+        g.vector.wait_ge(S["re%d" % (k + 1)], 1)
+        if k:
+            g.vector.wait_ge(S["ad%d" % (k - 1)], 1)
+        g.vector.tensor_tensor(o, a, T.relu[:, 256 * k + 256:256 * k + 512], AluOpType.add).then_inc(S["ad%d" % k], 1)
+    g.vector.wait_ge(S.pad, 1)
+    g.vector.wait_ge(S.ad4, 1)
+    g.vector.quantize_mx(T.qtc[:], T.qtp[:], T.tile[:]).then_inc(S.qt, 1)
+    g.wait_ge(S.qt, 1)
+    o = 256 * h + 64 * i
+    groups = {}
+    for r in T.cores:
+        groups.setdefault(_result_mask(topo, core, r, root), []).append(r)
+    sem = S["res%d" % h]
+    fused([(rs, m, codes(T.qtc, 0, 64), codes(T.rc, o, o + 64), sem) for m, rs in groups.items()])
+    fused([(rs, m, T.qtp[:, 0:64], T.rp[:, o:o + 64], sem) for m, rs in groups.items()])
+    g.wait_ge(S.sent, sent[0])
+
+
+def _result_mask(topo, site, r, root):
+    m = topo.mask(site, r)
+    if topo.chip(site) == topo.chip(r):
+        off = [topo.mask(site, c) for c in range(NCORES) if topo.chip(c) != topo.chip(site)][0]
+        m &= ~off
+    return m

@@ -11,22 +11,31 @@ SCRATCH = {
     "qsc": ("sbuf", [128, 512], F8), "qsp": ("sbuf", [128, 512], U8),
     "rc": ("sbuf", [128, 512], F8), "rp": ("sbuf", [128, 512], U8),
     "ysb": ("sbuf", [128, 2048], "float32"),
-    "ac": ("sbuf", [128, 768], F8), "ap": ("sbuf", [128, 768], U8),
-    "bc": ("sbuf", [128, 512], F8), "bp": ("sbuf", [128, 512], U8),
+    "yc": ("sbuf", [128, 256], F8), "yp": ("sbuf", [128, 256], U8),
+    "ic": ("sbuf", [128, 1280], F8), "ip": ("sbuf", [128, 1280], U8),
     "relu": ("sbuf", [128, 1536], "float32"),
     "acc": ("sbuf", [128, 1024], "float32"),
     "tile": ("sbuf", [128, 512], "bfloat16"),
     "qtc": ("sbuf", [128, 128], F8), "qtp": ("sbuf", [128, 128], U8),
     "ps": ("psum", [128, 4096], "float32"),
 }
-SEMAPHORES = (["la0", "la1", "lb0", "lb1", "ones", "onehot", "qa", "qb0", "qb1", "qs", "sent", "res0", "res1",
-               "cv0", "cv1", "cs0", "cs1", "st0", "st1", "a", "x", "b", "bf", "pad", "qt"]
-              + ["mm%d" % k for k in range(8)] + ["re%d" % k for k in range(6)] + ["ad%d" % k for k in range(5)])
+SEMAPHORES = (["la0", "la1", "lb0", "lb1", "ones", "onehot", "qa0", "qa1", "qb0", "qb1", "qs", "sent", "res0", "res1",
+               "b", "bfp", "bfc", "ryp", "ryc", "rap", "rac", "pad", "qt"]
+              + [p + "%d" % k for p in ("cv", "cs", "st") for k in range(5)]
+              + [p + "%d" % k for p in ("r", "re") for k in range(6)]
+              + ["mm%d" % k for k in range(8)] + ["ad%d" % k for k in range(5)])
 NCORES = 128
+NEAR_B, FAR_B = 640, 384
+FAR_RANK = [0, 1, 2, 0]
+STORES = [(0, 1), (1, 2), (2, 4), (4, 6), (6, 8)]
 
 
 def _bits(mask):
     return [1 << k for k in range(mask.bit_length()) if (mask >> k) & 1]
+
+
+def _nb(mask):
+    return len(_bits(mask))
 
 
 def _split(mask, n):
@@ -35,165 +44,228 @@ def _split(mask, n):
     return [sum(e[k * m:(k + 1) * m]) for k in range(n)]
 
 
-def _dst(topo, c):
-    rid, pid, _ = topo.addr(c)
-    return DstId(rid=rid, pnc=pid)
-
-
-def _plan(T, topo):
-    root = T.cores[T.root]
-    home = topo.chip(root)
-    gates = [c for c in range(NCORES) if c not in T.cores and all(topo.may_write(c, r) for r in T.cores)]
-    near = [c for c in gates if topo.chip(c) == home][:4]
-    far = [c for c in gates if topo.mates(topo.chip(c), home)]
-    pair = []
-    for c in near:
-        m = [f for f in far if topo.die(f) == topo.die(c) and f not in pair]
-        pair.append(m[0])
-    g0 = [r for r in T.cores if topo.may_write(r, near[0])]
-    g1 = [r for r in T.cores if r not in g0]
-    return root, near, pair, g0, g1
-
-
 def rank_program(g, core, T, topo):
-    root, near, far, g0, g1 = _plan(T, topo)
-    sites = [near, far]
     S = T.sem
+    root = T.cores[T.root]
+
+    def onchip(c, d):
+        return topo.chip(c) == topo.chip(d)
+
+    def off_mask(c):
+        return [topo.mask(c, d) for d in range(NCORES) if not onchip(c, d)][0]
+
+    def on_mask(c):
+        return [topo.mask(c, d) for d in range(NCORES) if d != c and onchip(c, d)][0]
+
+    def stay_mask(c):
+        return on_mask(c) & ~off_mask(c)
+
+    gates = [c for c in range(NCORES) if c not in T.cores and all(topo.may_write(c, r) for r in T.cores)]
+    near = [c for c in gates if onchip(c, root)][:4]
+    g0 = [r for r in T.cores if topo.may_write(r, near[0]) and r != root] + [root]
+    g1 = [r for r in T.cores if r not in g0]
+    far = []
+    for k in FAR_RANK:
+        c = [c for c in gates if onchip(c, g1[k]) and c not in far]
+        have = [topo.die(f) for f in far if onchip(f, g1[k])]
+        far.append([x for x in c if (topo.die(x) == topo.die(g1[k])) == (not have)][0])
+    sites = [near, far]
+    slots = g0 + g1
+
+    def place(r):
+        s = slots.index(r)
+        return 128 * s if s < len(g0) else NEAR_B + 256 + 128 * (s - len(g0))
+
+    def landed(r):
+        return S["r%d" % slots.index(r)]
+
+    def relays(r):
+        if r == root:
+            return []
+        gs = [c for c in gates if onchip(c, r)]
+        out = [([c for c in gs if c in far and far.index(c) // 2 == p] + [None])[0] for p in range(2)]
+        for p in range(2):
+            if out[p] is None:
+                o = out[1 - p]
+                d = topo.die(r) if o is None else 1 - topo.die(o)
+                out[p] = [c for c in gs if topo.die(c) == d][0]
+        return out
+
+    def direct(r):
+        d = [(c, i) for i, c in enumerate(near if r in g0 else far) if c not in relays(r)]
+        off = [x for x in d if not onchip(x[0], r)]
+        on = [x for x in d if onchip(x[0], r)]
+        out = []
+        if off:
+            out += [(c, m, i) for (c, i), m in zip(off, _split(off_mask(r), 4 if len(off) == 3 else len(off)))]
+        if on:
+            m = stay_mask(r) if off else on_mask(r)
+            out += [(c, m, i) for (c, i), m in zip(on, _split(m, len(on)))]
+        return out
+
+    def relayed(r, c):
+        p = relays(r).index(c)
+        to = far if r in g0 else near
+        return [(to[2 * p + k], m, 128 * k) for k, m in enumerate(_split(off_mask(c), 2))]
+
     sent = [0]
 
-    def codes(buf, a, b):
-        return buf[:, a:b].bitcast(dt.uint8)
+    def dst(c):
+        rid, pid, _ = topo.addr(c)
+        return DstId(rid=rid, pnc=pid)
 
-    def fused(parts):
-        g.remote_dma_fused([RemoteDMATransfer(dst_ids=[_dst(topo, d) for d in ds], dma_engine_mask=m, remote_sem=sem,
-                                              srcs=[src], dsts=[dst] * len(ds))
-                            for ds, m, src, dst, sem in parts], local_sem=S.sent)
-        sent[0] += sum(len(_bits(p[1])) for p in parts)
+    def send(w, parts, src, to, n):
+        def cut(k, a):
+            return k[1][:, a:a + n] if w else k[0][:, a:a + n].bitcast(dt.uint8)
+        g.remote_dma_fused([RemoteDMATransfer(dst_ids=[dst(c) for c in cs], dma_engine_mask=m, remote_sem=sem,
+                                              srcs=[cut(src, a)], dsts=[cut(to, o)] * len(cs))
+                            for cs, m, a, o, sem in parts], local_sem=S.sent)
+        sent[0] += sum(_nb(p[1]) for p in parts)
 
-    def a_masks(r):
-        to = near if r in g0 else far
-        return to, _split(topo.mask(r, to[0]), 4)
+    QA, QB, QT = (T.qac, T.qap), (T.qbc, T.qbp), (T.qtc, T.qtp)
+    Y, I, R = (T.yc, T.yp), (T.ic, T.ip), (T.rc, T.rp)
 
     if core in T.cores:
-        to, masks = a_masks(core)
-        slot = (g0 + g1).index(core)
-        g.sync.dma_start(T.at[:, 0:1024], T.a[:, 0:1024]).then_inc(S.la0, 16)
-        g.scalar.dma_start(T.at[:, 1024:2048], T.a[:, 1024:2048]).then_inc(S.la1, 16)
-        if core == root:
-            g.sync.dma_start(T.bt[:, 1024:2048], T.b[:, 1024:2048]).then_inc(S.lb1, 16)
-            g.scalar.dma_start(T.bt[:, 0:1024], T.b[:, 0:1024]).then_inc(S.lb0, 16)
+        la = [(g.sync, T.at, T.a, 0, S.la0), (g.scalar, T.at, T.a, 1024, S.la1)]
+        lb = [(g.sync, T.bt, T.b, 1024, S.lb1), (g.scalar, T.bt, T.b, 0, S.lb0)]
+        for q, d, s, o, sem in lb + la if core == root else la:
+            q.dma_start(d[:, o:o + 1024], s[:, o:o + 1024]).then_inc(sem, 16)
         g.vector.memset(T.sel[:], 1.0).then_inc(S.ones, 1)
-        for k, s in enumerate((S.la0, S.la1)):
-            g.vector.wait_ge(s, 16)
-            g.vector.quantize_mx(T.qac[:, 256 * k:256 * k + 256], T.qap[:, 256 * k:256 * k + 256],
-                                 T.at[:, 1024 * k:1024 * k + 1024]).then_inc(S.qa, 1)
+
+        def quant(k, w, q, t, done):
+            g.vector.wait_ge(w, 16)
+            g.vector.quantize_mx(q[0][:, k:k + 256], q[1][:, k:k + 256], t[:, 4 * k:4 * k + 1024]).then_inc(done, 1)
+
         if core == root:
-            for k, s, q in ((1, S.lb1, S.qb1), (0, S.lb0, S.qb0)):
-                g.vector.wait_ge(s, 16)
-                g.vector.quantize_mx(T.qbc[:, 256 * k:256 * k + 256], T.qbp[:, 256 * k:256 * k + 256],
-                                     T.bt[:, 1024 * k:1024 * k + 1024]).then_inc(q, 1)
-        g.wait_ge(S.qa, 2)
-        o = 128 * slot
-        fused([([to[i]], masks[i], codes(T.qac, 128 * i, 128 * i + 128), codes(T.ac, o, o + 128), S.a) for i in range(4)])
-        fused([([to[i]], masks[i], T.qap[:, 128 * i:128 * i + 128], T.ap[:, o:o + 128], S.a) for i in range(4)])
+            quant(256, S.lb1, QB, T.bt, S.qb1)
+            quant(0, S.lb0, QB, T.bt, S.qb0)
+        quant(0, S.la0, QA, T.at, S.qa0)
+        quant(256, S.la1, QA, T.at, S.qa1)
+        m, stay = on_mask(core), stay_mask(core)
         if core == root:
-            m = topo.mask(core, near[0])
-            for k, q, s in ((1, S.qb1, S.bf), (0, S.qb0, S.b)):
-                g.wait_ge(q, 1)
-                fused([(near, m, codes(T.qbc, 256 * k, 256 * k + 256), codes(T.bc, 256 * k, 256 * k + 256), s)])
-                fused([(near, m, T.qbp[:, 256 * k:256 * k + 256], T.bp[:, 256 * k:256 * k + 256], s)])
+            g.wait_ge(S.qb1, 1)
+            send(1, [(near, stay, 256, FAR_B, S.bfp)], QB, I, 256)
+            send(0, [(near, m, 256, FAR_B, S.bfc)], QB, I, 256)
+            g.wait_ge(S.qb0, 1)
+            for w in (1, 0):
+                send(w, [(near, m, 0, NEAR_B, S.b)], QB, I, 256)
+            g.wait_ge(S.qa0, 1)
+            g.wait_ge(S.qa1, 1)
+            sp, sc = S.rap, S.rac
+        else:
+            for p, c in enumerate(relays(core)):
+                g.wait_ge(S["qa%d" % p], 1)
+                send(1, [([c], stay, 256 * p, 0, S.ryp)], QA, Y, 256)
+            send(0, [([c], x, 256 * p, 0, S.ryc) for p, (c, x) in enumerate(zip(relays(core), _split(stay, 2)))], QA, Y, 256)
+            sp = sc = landed(core)
+        for w, s in ((1, sp), (0, sc)):
+            send(w, [([c], x, 128 * i, place(core), s) for c, x, i in direct(core)], QA, I, 128)
         g.wait_ge(S.ones, 1)
         g.affine_select(T.sel[:], T.sel[:], [[1, 4], [-1, 512]], AluOpType.is_equal, 0.0, 0, 4).then_inc(S.onehot, 1)
         g.vector.wait_ge(S.onehot, 1)
         g.vector.quantize_mx(T.qsc[:], T.qsp[:], T.sel[:]).then_inc(S.qs, 1)
         g.tensor.wait_ge(S.qs, 1)
-        for h in range(2):
-            need = 0
-            for c in sites[h]:
-                need += 2 * len(_bits(_result_mask(topo, c, core, root)))
-            g.tensor.wait_ge(S["res%d" % h], need)
-            for b in range(4):
-                k = 4 * h + b
-                g.tensor.matmul_mx(T.ps[:, 512 * k:512 * k + 256], T.qsc[:, 128 * b:128 * b + 128],
-                                   T.qsp[:, 128 * b:128 * b + 128], T.rc[:, 256 * h:256 * h + 256],
-                                   T.rp[:, 256 * h:256 * h + 256], True, True).then_inc(S["mm%d" % k], 1)
-        for h in range(2):
-            for b in range(4):
-                k = 4 * h + b
-                q = g.vector if b % 2 == 0 else g.scalar
+        for k in range(8):
+            h, b = divmod(k, 4)
+            if b == 0:
+                g.tensor.wait_ge(S["res%d" % h], sum(2 * _nb(off_mask(c)) for c in sites[h]))
+            g.tensor.matmul_mx(T.ps[:, 512 * k:512 * k + 256], T.qsc[:, 128 * b:128 * b + 128], T.qsp[:, 128 * b:128 * b + 128],
+                               T.rc[:, 256 * h:256 * h + 256], T.rp[:, 256 * h:256 * h + 256],
+                               True, True).then_inc(S["mm%d" % k], 1)
+        for n, (u, v) in enumerate(STORES):
+            nv = ns = 0
+            for k in range(u, v):
+                q = g.scalar if k % 2 else g.vector
                 q.wait_ge(S["mm%d" % k], 1)
                 for i in range(4):
-                    o = 1024 * h + 4 * b + i
-                    out = T.ysb[:, o:1024 * h + 1024:16]
-                    src = T.ps[:, 512 * k + 64 * i:512 * k + 64 * i + 64]
-                    if b % 2 == 0:
-                        g.vector.tensor_copy(out, src).then_inc(S["cv%d" % h], 1)
+                    out, src = T.ysb[:, 256 * k + i:256 * k + 256:4], T.ps[:, 512 * k + 64 * i:512 * k + 64 * i + 64]
+                    if k % 2:
+                        g.scalar.activation(out, src, AF.Copy).then_inc(S["cs%d" % n], 1)
+                        ns += 1
                     else:
-                        g.scalar.activation(out, src, AF.Copy).then_inc(S["cs%d" % h], 1)
-            d = g.sync if h == 0 else g.scalar
-            d.wait_ge(S["cv%d" % h], 8)
-            d.wait_ge(S["cs%d" % h], 8)
-            d.dma_start(T.y[:, 1024 * h:1024 * h + 1024], T.ysb[:, 1024 * h:1024 * h + 1024]).then_inc(S["st%d" % h], 16)
-            d.wait_ge(S["st%d" % h], 16)
+                        g.vector.tensor_copy(out, src).then_inc(S["cv%d" % n], 1)
+                        nv += 1
+            if nv:
+                g.sync.wait_ge(S["cv%d" % n], nv)
+            if ns:
+                g.sync.wait_ge(S["cs%d" % n], ns)
+            g.sync.dma_start(T.y[:, 256 * u:256 * v], T.ysb[:, 256 * u:256 * v]).then_inc(S["st%d" % n], 16)
+        for n in range(len(STORES)):
+            g.sync.wait_ge(S["st%d" % n], 16)
         g.wait_ge(S.sent, sent[0])
         return
 
-    if core not in near and core not in far:
+    through = {}
+    n_ryp = n_ryc = 0
+    for r in T.cores:
+        if core in relays(r):
+            n_ryp, n_ryc = _nb(stay_mask(r)), _nb(stay_mask(r)) // 2
+            for w, s, n in ((1, S.ryp, n_ryp), (0, S.ryc, n_ryc)):
+                g.wait_ge(s, n)
+                send(w, [([c], m, k, place(r), landed(r)) for c, m, k in relayed(r, core)], Y, I, 128)
+            if core in far:
+                through[r] = 128 * (far.index(core) % 2)
+    if core not in near + far:
+        if n_ryp:
+            g.wait_ge(S.sent, sent[0])
         return
+
     h = 0 if core in near else 1
     i = sites[h].index(core)
-    partner = sites[1 - h][i]
-    pm = topo.mask(core, partner)
-    own, other = (g0, g1) if h == 0 else (g1, g0)
-    n_a = sum(2 * len(_bits(a_masks(r)[1][i])) for r in own)
-    n_x = 2 * len(_bits(topo.mask(partner, core)))
-    n_b = 2 * len(_bits(topo.mask(root, core) if h == 0 else topo.mask(near[i], core)))
-    first = (0, 384) if h == 0 else (384, 768)
-    g.wait_ge(S.a, n_a)
-    fused([([partner], pm, codes(T.ac, *first), codes(T.ac, *first), S.x)])
-    fused([([partner], pm, T.ap[:, first[0]:first[1]], T.ap[:, first[0]:first[1]], S.x)])
+    m = off_mask(core)
+    due = {}
+    for r in T.cores:
+        due[r] = (sum(2 * _nb(x) for c, x, _ in direct(r) if c == core)
+                  + sum(2 * _nb(x) for p in relays(r) for c, x, _ in relayed(r, p) if c == core))
     if h == 0:
-        g.wait_ge(S.bf, n_b)
-        fused([([partner], pm, codes(T.bc, 256, 512), codes(T.bc, 256, 512), S.b)])
-        fused([([partner], pm, T.bp[:, 256:512], T.bp[:, 256:512], S.b)])
-    order = [(g0 + g1).index(r) for r in own + other]
+        n_b, n_ra = 2 * _nb(on_mask(root)), due[root] // 2
+        for w, s, n in ((1, S.bfp, _nb(stay_mask(root))), (0, S.bfc, _nb(on_mask(root)))):
+            g.wait_ge(s, n)
+            send(w, [([far[i]], m, FAR_B, FAR_B, S.b)], I, I, 256)
+        for w, s in ((1, S.rap), (0, S.rac)):
+            g.wait_ge(s, n_ra)
+            send(w, [([far[i]], m, place(root), place(root), s)], I, I, 128)
+    else:
+        n_ra = _nb(off_mask(near[i]))
+        n_b = 2 * n_ra
     g.tensor.wait_ge(S.b, n_b)
-    g.tensor.wait_ge(S.a, n_a)
-    for k, s in enumerate(order):
-        if k == len(own):
-            g.tensor.wait_ge(S.x, n_x)
-        g.tensor.matmul_mx(T.ps[:, 512 * k:512 * k + 256], T.ac[:, 128 * s:128 * s + 128], T.ap[:, 128 * s:128 * s + 128],
-                           T.bc[:, 256 * h:256 * h + 256], T.bp[:, 256 * h:256 * h + 256],
-                           True, True).then_inc(S["mm%d" % k], 1)
+    bo = NEAR_B if h == 0 else FAR_B
+    for k, r in enumerate(g0 + g1 if h == 0 else g1 + g0):
+        (wc, wp), o = (Y, through[r]) if r in through else (I, place(r))
+        if r == root:
+            g.tensor.wait_ge(S.rap, n_ra)
+            g.tensor.wait_ge(S.rac, n_ra)
+        elif r in through:
+            g.tensor.wait_ge(S.ryp, n_ryp)
+            g.tensor.wait_ge(S.ryc, n_ryc)
+        else:
+            g.tensor.wait_ge(landed(r), due[r])
+        g.tensor.matmul_mx(T.ps[:, 512 * k:512 * k + 256], wc[:, o:o + 128], wp[:, o:o + 128],
+                           T.ic[:, bo:bo + 256], T.ip[:, bo:bo + 256], True, True).then_inc(S["mm%d" % k], 1)
     for k in range(6):
         g.scalar.wait_ge(S["mm%d" % k], 1)
         g.scalar.activation(T.relu[:, 256 * k:256 * k + 256], T.ps[:, 512 * k:512 * k + 256], AF.Relu).then_inc(S["re%d" % k], 1)
     g.vector.memset(T.tile[:, 256:512], 0.0).then_inc(S.pad, 1)
     g.vector.wait_ge(S.re0, 1)
     for k in range(5):
-        a = T.relu[:, 0:256] if k == 0 else T.acc[:, 256 * k - 256:256 * k]
-        o = T.tile[:, 0:256] if k == 4 else T.acc[:, 256 * k:256 * k + 256]
+        a = T.relu if k == 0 else T.acc
+        o = 0 if k == 0 else 256 * k - 256
+        b = 256 * k + 256
         g.vector.wait_ge(S["re%d" % (k + 1)], 1)
         if k:
             g.vector.wait_ge(S["ad%d" % (k - 1)], 1)
-        g.vector.tensor_tensor(o, a, T.relu[:, 256 * k + 256:256 * k + 512], AluOpType.add).then_inc(S["ad%d" % k], 1)
+        if k < 4:
+            g.vector.tensor_tensor(T.acc[:, 256 * k:256 * k + 256], a[:, o:o + 256], T.relu[:, b:b + 256],
+                                   AluOpType.add).then_inc(S["ad%d" % k], 1)
+            continue
+        for t in range(4):
+            g.vector.tensor_tensor(T.tile[:, t:256:4], a[:, o + 64 * t:o + 64 * t + 64], T.relu[:, b + 64 * t:b + 64 * t + 64],
+                                   AluOpType.add).then_inc(S.ad4, 1)
     g.vector.wait_ge(S.pad, 1)
-    g.vector.wait_ge(S.ad4, 1)
+    g.vector.wait_ge(S.ad4, 4)
     g.vector.quantize_mx(T.qtc[:], T.qtp[:], T.tile[:]).then_inc(S.qt, 1)
     g.wait_ge(S.qt, 1)
-    o = 256 * h + 64 * i
-    groups = {}
-    for r in T.cores:
-        groups.setdefault(_result_mask(topo, core, r, root), []).append(r)
-    sem = S["res%d" % h]
-    fused([(rs, m, codes(T.qtc, 0, 64), codes(T.rc, o, o + 64), sem) for m, rs in groups.items()])
-    fused([(rs, m, T.qtp[:, 0:64], T.rp[:, o:o + 64], sem) for m, rs in groups.items()])
+    k = (4 * h + i) % len(T.cores)
+    for w in (0, 1):
+        send(w, [(T.cores[k:] + T.cores[:k], m, 0, 256 * h + 64 * i, S["res%d" % h])], QT, R, 64)
     g.wait_ge(S.sent, sent[0])
-
-
-def _result_mask(topo, site, r, root):
-    m = topo.mask(site, r)
-    if topo.chip(site) == topo.chip(r):
-        off = [topo.mask(site, c) for c in range(NCORES) if topo.chip(c) != topo.chip(site)][0]
-        m &= ~off
-    return m

@@ -5,29 +5,33 @@ F8, U8 = "float8_e4m3fn_x4", "uint8"
 SCRATCH = {
     "at": ("sbuf", [128, 2048], "bfloat16"),
     "bt": ("sbuf", [128, 2048], "bfloat16"),
-    "sel": ("sbuf", [128, 2048], "bfloat16"),
     "qac": ("sbuf", [128, 512], F8), "qap": ("sbuf", [128, 512], U8),
     "qbc": ("sbuf", [128, 512], F8), "qbp": ("sbuf", [128, 512], U8),
     "qsc": ("sbuf", [128, 512], F8), "qsp": ("sbuf", [128, 512], U8),
     "rc": ("sbuf", [128, 512], F8), "rp": ("sbuf", [128, 512], U8),
     "ysb": ("sbuf", [128, 2048], "float32"),
-    "yc": ("sbuf", [128, 256], F8), "yp": ("sbuf", [128, 256], U8),
-    "ic": ("sbuf", [128, 1280], F8), "ip": ("sbuf", [128, 1280], U8),
-    "relu": ("sbuf", [128, 1536], "float32"),
-    "acc": ("sbuf", [128, 1024], "float32"),
+    "sel": ("sbuf", [128, 512], "bfloat16"),
+    "qmc": ("sbuf", [128, 128], F8), "qmp": ("sbuf", [128, 128], U8),
+    "yc": ("sbuf", [128, 128], F8), "yp": ("sbuf", [128, 128], U8),
+    "fc": ("sbuf", [128, 128], F8), "fp": ("sbuf", [128, 128], U8),
+    "ic": ("sbuf", [128, 768], F8), "ip": ("sbuf", [128, 768], U8),
+    "bc": ("sbuf", [128, 256], F8), "bp": ("sbuf", [128, 256], U8),
+    "relu": ("sbuf", [128, 1280], "bfloat16"),
+    "keep": ("sbuf", [128, 1280], "bfloat16"),
+    "acc": ("sbuf", [128, 1280], "bfloat16"),
+    "last": ("sbuf", [128, 256], "bfloat16"),
     "tile": ("sbuf", [128, 512], "bfloat16"),
     "qtc": ("sbuf", [128, 128], F8), "qtp": ("sbuf", [128, 128], U8),
     "ps": ("psum", [128, 4096], "float32"),
 }
 SEMAPHORES = (["la0", "la1", "lb0", "lb1", "ones", "onehot", "qa0", "qa1", "qb0", "qb1", "qs", "sent", "res0", "res1",
-               "b", "bfp", "bfc", "ryp", "ryc", "rap", "rac", "pad", "qt"]
-              + [p + "%d" % k for p in ("cv", "cs", "st") for k in range(5)]
+               "sm", "b", "bfp", "bfc", "ryp", "ryc", "pad", "qt", "msk", "sum", "tl"]
+              + [p + "%d" % k for p in ("cv", "cs", "st") for k in range(6)]
               + [p + "%d" % k for p in ("r", "re") for k in range(6)]
-              + ["mm%d" % k for k in range(8)] + ["ad%d" % k for k in range(5)])
+              + ["mm%d" % k for k in range(8)])
 NCORES = 128
-NEAR_B, FAR_B = 640, 384
-FAR_RANK = [0, 1, 2, 0]
-STORES = [(0, 1), (1, 2), (2, 4), (4, 6), (6, 8)]
+HOME = [[0, 0, 1, 2], [0, 1, 2, 0]]
+STORES = [(0, 1), (1, 2), (2, 4), (4, 5), (5, 6), (6, 8)]
 
 
 def _bits(mask):
@@ -60,53 +64,40 @@ def rank_program(g, core, T, topo):
     def stay_mask(c):
         return on_mask(c) & ~off_mask(c)
 
+    def few(c):
+        return _split(stay_mask(c), 2)[0]
+
     gates = [c for c in range(NCORES) if c not in T.cores and all(topo.may_write(c, r) for r in T.cores)]
-    near = [c for c in gates if onchip(c, root)][:4]
-    g0 = [r for r in T.cores if topo.may_write(r, near[0]) and r != root] + [root]
+    g0 = [root] + [r for r in T.cores if r != root and topo.same_plane(topo.chip(r), topo.chip(root))]
     g1 = [r for r in T.cores if r not in g0]
-    far = []
-    for k in FAR_RANK:
-        c = [c for c in gates if onchip(c, g1[k]) and c not in far]
-        have = [topo.die(f) for f in far if onchip(f, g1[k])]
-        far.append([x for x in c if (topo.die(x) == topo.die(g1[k])) == (not have)][0])
-    sites = [near, far]
-    slots = g0 + g1
+    planes = [g0, g1]
+    sites = [[], []]
+    for h in range(2):
+        for i in range(4):
+            r = planes[h][HOME[h][i]]
+            have = [topo.die(s) for s in sites[h] if onchip(s, r)]
+            d = 1 - have[0] if have else 1 - i % 2
+            sites[h].append([c for c in gates if onchip(c, r) and c not in sites[h] and topo.die(c) == d][0])
+    relay = {}
+    for r in T.cores:
+        h = 0 if r in g0 else 1
+        free = [c for c in gates if onchip(c, r) and c not in sites[h]]
+        relay[r] = [s if onchip(s, r) else free.pop(0) for s in sites[h]]
+    order = g0 + g1
 
     def place(r):
-        s = slots.index(r)
-        return 128 * s if s < len(g0) else NEAR_B + 256 + 128 * (s - len(g0))
+        return 128 * order.index(r)
 
     def landed(r):
-        return S["r%d" % slots.index(r)]
-
-    def relays(r):
-        if r == root:
-            return []
-        gs = [c for c in gates if onchip(c, r)]
-        out = [([c for c in gs if c in far and far.index(c) // 2 == p] + [None])[0] for p in range(2)]
-        for p in range(2):
-            if out[p] is None:
-                o = out[1 - p]
-                d = topo.die(r) if o is None else 1 - topo.die(o)
-                out[p] = [c for c in gs if topo.die(c) == d][0]
-        return out
+        return S["r%d" % order.index(r)]
 
     def direct(r):
-        d = [(c, i) for i, c in enumerate(near if r in g0 else far) if c not in relays(r)]
-        off = [x for x in d if not onchip(x[0], r)]
-        on = [x for x in d if onchip(x[0], r)]
-        out = []
-        if off:
-            out += [(c, m, i) for (c, i), m in zip(off, _split(off_mask(r), 4 if len(off) == 3 else len(off)))]
-        if on:
-            m = stay_mask(r) if off else on_mask(r)
-            out += [(c, m, i) for (c, i), m in zip(on, _split(m, len(on)))]
-        return out
+        h = 0 if r in g0 else 1
+        d = [(c, i) for i, c in enumerate(sites[h]) if not onchip(c, r)]
+        return [(c, m, i) for (c, i), m in zip(d, _split(off_mask(r), 4 if len(d) == 3 else len(d)))]
 
-    def relayed(r, c):
-        p = relays(r).index(c)
-        to = far if r in g0 else near
-        return [(to[2 * p + k], m, 128 * k) for k, m in enumerate(_split(off_mask(c), 2))]
+    def bfar(q):
+        return sites[1][2 * (q // 2):2 * (q // 2) + 2]
 
     sent = [0]
 
@@ -117,20 +108,20 @@ def rank_program(g, core, T, topo):
     def send(w, parts, src, to, n):
         def cut(k, a):
             return k[1][:, a:a + n] if w else k[0][:, a:a + n].bitcast(dt.uint8)
+        parts = [p for p in parts if p[0]]
         g.remote_dma_fused([RemoteDMATransfer(dst_ids=[dst(c) for c in cs], dma_engine_mask=m, remote_sem=sem,
                                               srcs=[cut(src, a)], dsts=[cut(to, o)] * len(cs))
                             for cs, m, a, o, sem in parts], local_sem=S.sent)
         sent[0] += sum(_nb(p[1]) for p in parts)
 
-    QA, QB, QT = (T.qac, T.qap), (T.qbc, T.qbp), (T.qtc, T.qtp)
-    Y, I, R = (T.yc, T.yp), (T.ic, T.ip), (T.rc, T.rp)
+    QA, QB, QT, QM, QS = (T.qac, T.qap), (T.qbc, T.qbp), (T.qtc, T.qtp), (T.qmc, T.qmp), (T.qsc, T.qsp)
+    Y, F, I, B, R = (T.yc, T.yp), (T.fc, T.fp), (T.ic, T.ip), (T.bc, T.bp), (T.rc, T.rp)
 
     if core in T.cores:
         la = [(g.sync, T.at, T.a, 0, S.la0), (g.scalar, T.at, T.a, 1024, S.la1)]
         lb = [(g.sync, T.bt, T.b, 1024, S.lb1), (g.scalar, T.bt, T.b, 0, S.lb0)]
         for q, d, s, o, sem in lb + la if core == root else la:
             q.dma_start(d[:, o:o + 1024], s[:, o:o + 1024]).then_inc(sem, 16)
-        g.vector.memset(T.sel[:], 1.0).then_inc(S.ones, 1)
 
         def quant(k, w, q, t, done):
             g.vector.wait_ge(w, 16)
@@ -141,34 +132,28 @@ def rank_program(g, core, T, topo):
             quant(0, S.lb0, QB, T.bt, S.qb0)
         quant(0, S.la0, QA, T.at, S.qa0)
         quant(256, S.la1, QA, T.at, S.qa1)
-        m, stay = on_mask(core), stay_mask(core)
+        m, off, stay = on_mask(core), off_mask(core), stay_mask(core)
         if core == root:
             g.wait_ge(S.qb1, 1)
-            send(1, [(near, stay, 256, FAR_B, S.bfp)], QB, I, 256)
-            send(0, [(near, m, 256, FAR_B, S.bfc)], QB, I, 256)
+            for w, s, x in ((1, S.bfp, off), (0, S.bfc, m)):
+                send(w, [([relay[root][j], relay[root][2 + j]], y, 256 + 128 * j, 0, s) for j, y in enumerate(_split(x, 2))],
+                     QB, F, 128)
             g.wait_ge(S.qb0, 1)
             for w in (1, 0):
-                send(w, [(near, m, 0, NEAR_B, S.b)], QB, I, 256)
-            g.wait_ge(S.qa0, 1)
-            g.wait_ge(S.qa1, 1)
-            sp, sc = S.rap, S.rac
-        else:
-            for p, c in enumerate(relays(core)):
-                g.wait_ge(S["qa%d" % p], 1)
-                send(1, [([c], stay, 256 * p, 0, S.ryp)], QA, Y, 256)
-            send(0, [([c], x, 256 * p, 0, S.ryc) for p, (c, x) in enumerate(zip(relays(core), _split(stay, 2)))], QA, Y, 256)
-            sp = sc = landed(core)
-        for w, s in ((1, sp), (0, sc)):
-            send(w, [([c], x, 128 * i, place(core), s) for c, x, i in direct(core)], QA, I, 128)
-        g.wait_ge(S.ones, 1)
-        g.affine_select(T.sel[:], T.sel[:], [[1, 4], [-1, 512]], AluOpType.is_equal, 0.0, 0, 4).then_inc(S.onehot, 1)
-        g.vector.wait_ge(S.onehot, 1)
-        g.vector.quantize_mx(T.qsc[:], T.qsp[:], T.sel[:]).then_inc(S.qs, 1)
-        g.tensor.wait_ge(S.qs, 1)
+                send(w, [([c for c in sites[0] if not onchip(c, root)], off, 0, 0, S.b),
+                         ([c for c in sites[0] if onchip(c, root)], stay, 0, 0, S.b)], QB, B, 256)
+        for p in range(2):
+            g.wait_ge(S["qa%d" % p], 1)
+            for w, s in ((1, S.ryp), (0, S.ryc)):
+                send(w, [([relay[core][2 * p + k]], y, 128 * (2 * p + k), 0, s) for k, y in enumerate(_split(stay, 2))],
+                     QA, Y, 128)
+        for w in (1, 0):
+            send(w, [([c], x, 128 * i, place(core), landed(core)) for c, x, i in direct(core)], QA, I, 128)
+        g.tensor.wait_ge(S.sm, sum(_nb(few(c)) + _nb(off_mask(c)) for c in relay[core]))
         for k in range(8):
             h, b = divmod(k, 4)
             if b == 0:
-                g.tensor.wait_ge(S["res%d" % h], sum(2 * _nb(off_mask(c)) for c in sites[h]))
+                g.tensor.wait_ge(S["res%d" % h], sum(2 * _nb(few(c) if onchip(c, core) else off_mask(c)) for c in sites[h]))
             g.tensor.matmul_mx(T.ps[:, 512 * k:512 * k + 256], T.qsc[:, 128 * b:128 * b + 128], T.qsp[:, 128 * b:128 * b + 128],
                                T.rc[:, 256 * h:256 * h + 256], T.rp[:, 256 * h:256 * h + 256],
                                True, True).then_inc(S["mm%d" % k], 1)
@@ -195,77 +180,73 @@ def rank_program(g, core, T, topo):
         g.wait_ge(S.sent, sent[0])
         return
 
-    through = {}
-    n_ryp = n_ryc = 0
-    for r in T.cores:
-        if core in relays(r):
-            n_ryp, n_ryc = _nb(stay_mask(r)), _nb(stay_mask(r)) // 2
-            for w, s, n in ((1, S.ryp, n_ryp), (0, S.ryc, n_ryc)):
-                g.wait_ge(s, n)
-                send(w, [([c], m, k, place(r), landed(r)) for c, m, k in relayed(r, core)], Y, I, 128)
-            if core in far:
-                through[r] = 128 * (far.index(core) % 2)
-    if core not in near + far:
-        if n_ryp:
-            g.wait_ge(S.sent, sent[0])
+    mine = [r for r in T.cores if core in relay[r]]
+    if not mine:
+        return
+    r = mine[0]
+    i = relay[r].index(core)
+    off = off_mask(core)
+    g.vector.memset(T.sel[:], 1.0).then_inc(S.ones, 1)
+    g.wait_ge(S.ones, 1)
+    g.affine_select(T.sel[:], T.sel[:], [[-1, 512]], AluOpType.is_equal, 0.0, i, 4).then_inc(S.onehot, 1)
+    g.vector.wait_ge(S.onehot, 1)
+    g.vector.quantize_mx(T.qmc[:], T.qmp[:], T.sel[:]).then_inc(S.qs, 1)
+    g.wait_ge(S.qs, 1)
+    for w, m in ((1, few(core)), (0, off)):
+        send(w, [([r], m, 0, 128 * i, S.sm)], QM, QS, 128)
+    if r == root:
+        for w, s, n in ((1, S.bfp, _nb(off_mask(root)) // 2), (0, S.bfc, _nb(on_mask(root)) // 2)):
+            g.wait_ge(s, n)
+            send(w, [(bfar(i), off, 0, 128 * (i % 2), S.b)], F, B, 128)
+    h = 0 if r in g0 else 1
+    n_ry = _nb(stay_mask(r)) // 2
+    for w, s in ((1, S.ryp), (0, S.ryc)):
+        g.wait_ge(s, n_ry)
+        send(w, [([sites[1 - h][i]], off, 0, place(r), landed(r))], Y, I, 128)
+    if core not in sites[h]:
+        g.wait_ge(S.sent, sent[0])
         return
 
-    h = 0 if core in near else 1
-    i = sites[h].index(core)
-    m = off_mask(core)
-    due = {}
-    for r in T.cores:
-        due[r] = (sum(2 * _nb(x) for c, x, _ in direct(r) if c == core)
-                  + sum(2 * _nb(x) for p in relays(r) for c, x, _ in relayed(r, p) if c == core))
     if h == 0:
-        n_b, n_ra = 2 * _nb(on_mask(root)), due[root] // 2
-        for w, s, n in ((1, S.bfp, _nb(stay_mask(root))), (0, S.bfc, _nb(on_mask(root)))):
-            g.wait_ge(s, n)
-            send(w, [([far[i]], m, FAR_B, FAR_B, S.b)], I, I, 256)
-        for w, s in ((1, S.rap), (0, S.rac)):
-            g.wait_ge(s, n_ra)
-            send(w, [([far[i]], m, place(root), place(root), s)], I, I, 128)
+        n_b = 2 * _nb(stay_mask(root) if r == root else off_mask(root))
     else:
-        n_ra = _nb(off_mask(near[i]))
-        n_b = 2 * n_ra
+        n_b = sum(2 * _nb(off_mask(c)) for q, c in enumerate(relay[root]) if core in bfar(q))
     g.tensor.wait_ge(S.b, n_b)
-    bo = NEAR_B if h == 0 else FAR_B
-    for k, r in enumerate(g0 + g1 if h == 0 else g1 + g0):
-        (wc, wp), o = (Y, through[r]) if r in through else (I, place(r))
-        if r == root:
-            g.tensor.wait_ge(S.rap, n_ra)
-            g.tensor.wait_ge(S.rac, n_ra)
-        elif r in through:
-            g.tensor.wait_ge(S.ryp, n_ryp)
-            g.tensor.wait_ge(S.ryc, n_ryc)
+    seq = [x for x in planes[h] if x != root] + planes[1 - h][::-1] + ([root] if h == 0 else [])
+    for k, x in enumerate(seq):
+        (wc, wp), o = (Y, 0) if x == r else (I, place(x))
+        if x == r:
+            g.tensor.wait_ge(S.ryp, n_ry)
+            g.tensor.wait_ge(S.ryc, n_ry)
+        elif x in planes[h]:
+            g.tensor.wait_ge(landed(x), sum(2 * _nb(m) for c, m, _ in direct(x) if c == core))
         else:
-            g.tensor.wait_ge(landed(r), due[r])
+            g.tensor.wait_ge(landed(x), 2 * _nb(off_mask(relay[x][i])))
         g.tensor.matmul_mx(T.ps[:, 512 * k:512 * k + 256], wc[:, o:o + 128], wp[:, o:o + 128],
-                           T.ic[:, bo:bo + 256], T.ip[:, bo:bo + 256], True, True).then_inc(S["mm%d" % k], 1)
+                           T.bc[:], T.bp[:], True, True).then_inc(S["mm%d" % k], 1)
     for k in range(6):
         g.scalar.wait_ge(S["mm%d" % k], 1)
-        g.scalar.activation(T.relu[:, 256 * k:256 * k + 256], T.ps[:, 512 * k:512 * k + 256], AF.Relu).then_inc(S["re%d" % k], 1)
+        out = T.relu[:, k:1280:5] if k < 5 else T.last[:]
+        g.scalar.activation(out, T.ps[:, 512 * k:512 * k + 256], AF.Relu).then_inc(S["re%d" % k], 1)
     g.vector.memset(T.tile[:, 256:512], 0.0).then_inc(S.pad, 1)
-    g.vector.wait_ge(S.re0, 1)
+    g.vector.memset(T.keep[:], 1.0).then_inc(S.pad, 1)
+    g.vector.wait_ge(S.pad, 2)
+    g.vector.memset(T.keep[:, 0:1280:5], 0.0).then_inc(S.msk, 1)
+    g.vector.wait_ge(S.msk, 1)
     for k in range(5):
-        a = T.relu if k == 0 else T.acc
-        o = 0 if k == 0 else 256 * k - 256
-        b = 256 * k + 256
-        g.vector.wait_ge(S["re%d" % (k + 1)], 1)
-        if k:
-            g.vector.wait_ge(S["ad%d" % (k - 1)], 1)
-        if k < 4:
-            g.vector.tensor_tensor(T.acc[:, 256 * k:256 * k + 256], a[:, o:o + 256], T.relu[:, b:b + 256],
-                                   AluOpType.add).then_inc(S["ad%d" % k], 1)
-            continue
-        for t in range(4):
-            g.vector.tensor_tensor(T.tile[:, t:256:4], a[:, o + 64 * t:o + 64 * t + 64], T.relu[:, b + 64 * t:b + 64 * t + 64],
-                                   AluOpType.add).then_inc(S.ad4, 1)
-    g.vector.wait_ge(S.pad, 1)
-    g.vector.wait_ge(S.ad4, 4)
+        g.vector.wait_ge(S["re%d" % k], 1)
+    g.vector.tensor_tensor_scan(T.acc[:], T.keep[:], T.relu[:], 0.0, AluOpType.mult, AluOpType.add).then_inc(S.sum, 1)
+    g.vector.wait_ge(S.sum, 1)
+    g.vector.wait_ge(S.re5, 1)
+    for t in range(4):
+        g.vector.tensor_tensor(T.tile[:, t:256:4], T.acc[:, 320 * t + 4:320 * t + 320:5], T.last[:, 64 * t:64 * t + 64],
+                               AluOpType.add).then_inc(S.tl, 1)
+    g.vector.wait_ge(S.tl, 4)
     g.vector.quantize_mx(T.qtc[:], T.qtp[:], T.tile[:]).then_inc(S.qt, 1)
     g.wait_ge(S.qt, 1)
     k = (4 * h + i) % len(T.cores)
+    to = T.cores[k:] + T.cores[:k]
     for w in (0, 1):
-        send(w, [(T.cores[k:] + T.cores[:k], m, 0, 256 * h + 64 * i, S["res%d" % h])], QT, R, 64)
+        send(w, [([c for c in to if onchip(c, core) == on], m, 0, 256 * h + 64 * i, S["res%d" % h])
+                 for on, m in ((False, off), (True, few(core)))], QT, R, 64)
     g.wait_ge(S.sent, sent[0])

@@ -14,6 +14,7 @@ SCRATCH = {
     "qmc": ("sbuf", [128, 128], F8), "qmp": ("sbuf", [128, 128], U8),
     "yc": ("sbuf", [128, 128], F8), "yp": ("sbuf", [128, 128], U8),
     "fc": ("sbuf", [128, 128], F8), "fp": ("sbuf", [128, 128], U8),
+    "hc": ("sbuf", [128, 64], F8), "hp": ("sbuf", [128, 64], U8),
     "ic": ("sbuf", [128, 768], F8), "ip": ("sbuf", [128, 768], U8),
     "bc": ("sbuf", [128, 256], F8), "bp": ("sbuf", [128, 256], U8),
     "relu": ("sbuf", [128, 1280], "bfloat16"),
@@ -24,14 +25,18 @@ SCRATCH = {
     "qtc": ("sbuf", [128, 128], F8), "qtp": ("sbuf", [128, 128], U8),
     "ps": ("psum", [128, 4096], "float32"),
 }
-SEMAPHORES = (["la0", "la1", "lb0", "lb1", "ones", "onehot", "qa0", "qa1", "qb0", "qb1", "qs", "sent", "res0", "res1",
+SEMAPHORES = (["la0", "la1", "lb0", "lb1", "ones", "onehot", "qa0", "qa1", "qb0", "qb1", "qs", "sent", "hlc", "hlp",
                "sm", "b", "bfp", "bfc", "ryp", "ryc", "pad", "qt", "msk", "sum", "tl"]
-              + [p + "%d" % k for p in ("cv", "cs", "st") for k in range(6)]
-              + [p + "%d" % k for p in ("r", "re") for k in range(6)]
-              + ["mm%d" % k for k in range(8)])
+              + ["res%d" % k for k in range(4)] + ["st%d" % k for k in range(6)]
+              + [p + "%d" % k for p in ("r", "re", "mm") for k in range(7)]
+              + [p + "%d" % k for p in ("mx", "cx") for k in range(16)])
 NCORES = 128
 HOME = [[0, 0, 1, 2], [0, 1, 2, 0]]
-STORES = [(0, 1), (1, 2), (2, 4), (4, 5), (5, 6), (6, 8)]
+FIRST = [3, 0]
+HELPED = 2
+STORES = [[(0, 2), (2, 4)], [(0, 1), (1, 2), (2, 3), (3, 4)]]
+BY_SCALAR = [(1, 3), (1, 3), (1, 3), (1,)]
+VECTOR_TERMS = (1, 3)
 
 
 def _bits(mask):
@@ -67,6 +72,9 @@ def rank_program(g, core, T, topo):
     def few(c):
         return _split(stay_mask(c), 2)[0]
 
+    def rest(c):
+        return _split(stay_mask(c), 2)[1]
+
     gates = [c for c in range(NCORES) if c not in T.cores and all(topo.may_write(c, r) for r in T.cores)]
     g0 = [root] + [r for r in T.cores if r != root and topo.same_plane(topo.chip(r), topo.chip(root))]
     g1 = [r for r in T.cores if r not in g0]
@@ -78,12 +86,24 @@ def rank_program(g, core, T, topo):
             have = [topo.die(s) for s in sites[h] if onchip(s, r)]
             d = 1 - have[0] if have else 1 - i % 2
             sites[h].append([c for c in gates if onchip(c, r) and c not in sites[h] and topo.die(c) == d][0])
+    products = sites[0] + sites[1]
     relay = {}
     for r in T.cores:
         h = 0 if r in g0 else 1
         free = [c for c in gates if onchip(c, r) and c not in sites[h]]
-        relay[r] = [s if onchip(s, r) else free.pop(0) for s in sites[h]]
+        crowd = [len([s for s in sites[1 - h] if onchip(s, t)]) for t in sites[1 - h]]
+        relay[r] = [s if onchip(s, r) else None for s in sites[h]]
+        for i in sorted(range(4), key=lambda k: -crowd[k]):
+            if relay[r][i] is None:
+                fit = [c for c in free if (topo.die(c) != topo.die(r)) == (crowd[i] > 1)] or free
+                relay[r][i] = fit[0]
+                free.remove(fit[0])
+    helper = {}
+    for p in products:
+        free = [c for c in gates if onchip(c, p) and c not in products and c not in helper.values()]
+        helper[p] = ([c for c in free if topo.die(c) != topo.die(p)] or free)[0]
     order = g0 + g1
+    near = [c for c in sites[0] if onchip(c, root)]
 
     def place(r):
         return 128 * order.index(r)
@@ -99,83 +119,100 @@ def rank_program(g, core, T, topo):
     def bfar(q):
         return sites[1][2 * (q // 2):2 * (q // 2) + 2]
 
+    def whose(p):
+        h = 0 if p in sites[0] else 1
+        return h, sites[h].index(p)
+
+    def targets(p):
+        k = FIRST[whose(p)[0]]
+        to = T.cores[k:] + T.cores[:k]
+        out = [c for c in to if not onchip(c, p)]
+        return out[:-HELPED], out[-HELPED:], [c for c in to if onchip(c, p)]
+
+    def result(p):
+        h, i = whose(p)
+        return 256 * h + 64 * i, S["res%d" % (2 * h + i // 2)]
+
     sent = [0]
 
     def dst(c):
         rid, pid, _ = topo.addr(c)
         return DstId(rid=rid, pnc=pid)
 
-    def send(w, parts, src, to, n):
+    def send(w, parts, src, n):
         def cut(k, a):
             return k[1][:, a:a + n] if w else k[0][:, a:a + n].bitcast(dt.uint8)
         parts = [p for p in parts if p[0]]
         g.remote_dma_fused([RemoteDMATransfer(dst_ids=[dst(c) for c in cs], dma_engine_mask=m, remote_sem=sem,
                                               srcs=[cut(src, a)], dsts=[cut(to, o)] * len(cs))
-                            for cs, m, a, o, sem in parts], local_sem=S.sent)
+                            for cs, m, a, to, o, sem in parts], local_sem=S.sent)
         sent[0] += sum(_nb(p[1]) for p in parts)
 
     QA, QB, QT, QM, QS = (T.qac, T.qap), (T.qbc, T.qbp), (T.qtc, T.qtp), (T.qmc, T.qmp), (T.qsc, T.qsp)
-    Y, F, I, B, R = (T.yc, T.yp), (T.fc, T.fp), (T.ic, T.ip), (T.bc, T.bp), (T.rc, T.rp)
+    Y, F, I, B, R, H = (T.yc, T.yp), (T.fc, T.fp), (T.ic, T.ip), (T.bc, T.bp), (T.rc, T.rp), (T.hc, T.hp)
 
     if core in T.cores:
-        la = [(g.sync, T.at, T.a, 0, S.la0), (g.scalar, T.at, T.a, 1024, S.la1)]
-        lb = [(g.sync, T.bt, T.b, 1024, S.lb1), (g.scalar, T.bt, T.b, 0, S.lb0)]
-        for q, d, s, o, sem in lb + la if core == root else la:
-            q.dma_start(d[:, o:o + 1024], s[:, o:o + 1024]).then_inc(sem, 16)
+        loads = [(T.at, T.a, 0, 1024, S.la0), (T.at, T.a, 1024, 1024, S.la1)]
+        if core == root:
+            loads = [(T.bt, T.b, o, 512, S.lb1 if o >= 1024 else S.lb0) for o in (1024, 1536, 0, 512)] + loads
+        for k, (d, s, o, n, sem) in enumerate(loads):
+            (g.scalar if k % 2 else g.sync).dma_start(d[:, o:o + n], s[:, o:o + n]).then_inc(sem, 16)
 
-        def quant(k, w, q, t, done):
-            g.vector.wait_ge(w, 16)
+        def quant(k, w, n, q, t, done):
+            g.vector.wait_ge(w, n)
             g.vector.quantize_mx(q[0][:, k:k + 256], q[1][:, k:k + 256], t[:, 4 * k:4 * k + 1024]).then_inc(done, 1)
 
         if core == root:
-            quant(256, S.lb1, QB, T.bt, S.qb1)
-            quant(0, S.lb0, QB, T.bt, S.qb0)
-        quant(0, S.la0, QA, T.at, S.qa0)
-        quant(256, S.la1, QA, T.at, S.qa1)
+            quant(256, S.lb1, 32, QB, T.bt, S.qb1)
+            quant(0, S.lb0, 32, QB, T.bt, S.qb0)
+        quant(0, S.la0, 16, QA, T.at, S.qa0)
+        quant(256, S.la1, 16, QA, T.at, S.qa1)
         m, off, stay = on_mask(core), off_mask(core), stay_mask(core)
         if core == root:
             g.wait_ge(S.qb1, 1)
             for w, s, x in ((1, S.bfp, off), (0, S.bfc, m)):
-                send(w, [([relay[root][j], relay[root][2 + j]], y, 256 + 128 * j, 0, s) for j, y in enumerate(_split(x, 2))],
-                     QB, F, 128)
+                send(w, [([relay[root][j], relay[root][2 + j]], y, 256 + 128 * j, F, 0, s)
+                         for j, y in enumerate(_split(x, 2))], QB, 128)
             g.wait_ge(S.qb0, 1)
             for w in (1, 0):
-                send(w, [([c for c in sites[0] if not onchip(c, root)], off, 0, 0, S.b),
-                         ([c for c in sites[0] if onchip(c, root)], stay, 0, 0, S.b)], QB, B, 256)
+                send(w, [([c for c in sites[0] if not onchip(c, root)], off, 0, B, 0, S.b),
+                         (near[:1], stay, 0, B, 0, S.b)], QB, 256)
         for p in range(2):
             g.wait_ge(S["qa%d" % p], 1)
             for w, s in ((1, S.ryp), (0, S.ryc)):
-                send(w, [([relay[core][2 * p + k]], y, 128 * (2 * p + k), 0, s) for k, y in enumerate(_split(stay, 2))],
-                     QA, Y, 128)
+                send(w, [([relay[core][2 * p + k]], y, 128 * (2 * p + k), Y, 0, s) for k, y in enumerate(_split(stay, 2))],
+                     QA, 128)
         for w in (1, 0):
-            send(w, [([c], x, 128 * i, place(core), landed(core)) for c, x, i in direct(core)], QA, I, 128)
+            send(w, [([c], x, 128 * i, I, place(core), landed(core)) for c, x, i in direct(core)], QA, 128)
+
+        me = T.cores.index(core)
+        halves = sorted(range(2), key=lambda h: (me - FIRST[h]) % len(T.cores))
         g.tensor.wait_ge(S.sm, sum(_nb(few(c)) + _nb(off_mask(c)) for c in relay[core]))
-        for k in range(8):
-            h, b = divmod(k, 4)
-            if b == 0:
-                g.tensor.wait_ge(S["res%d" % h], sum(2 * _nb(few(c) if onchip(c, core) else off_mask(c)) for c in sites[h]))
-            g.tensor.matmul_mx(T.ps[:, 512 * k:512 * k + 256], T.qsc[:, 128 * b:128 * b + 128], T.qsp[:, 128 * b:128 * b + 128],
-                               T.rc[:, 256 * h:256 * h + 256], T.rp[:, 256 * h:256 * h + 256],
-                               True, True).then_inc(S["mm%d" % k], 1)
-        for n, (u, v) in enumerate(STORES):
-            nv = ns = 0
-            for k in range(u, v):
-                q = g.scalar if k % 2 else g.vector
-                q.wait_ge(S["mm%d" % k], 1)
-                for i in range(4):
-                    out, src = T.ysb[:, 256 * k + i:256 * k + 256:4], T.ps[:, 512 * k + 64 * i:512 * k + 64 * i + 64]
-                    if k % 2:
-                        g.scalar.activation(out, src, AF.Copy).then_inc(S["cs%d" % n], 1)
-                        ns += 1
-                    else:
-                        g.vector.tensor_copy(out, src).then_inc(S["cv%d" % n], 1)
-                        nv += 1
-            if nv:
-                g.sync.wait_ge(S["cv%d" % n], nv)
-            if ns:
-                g.sync.wait_ge(S["cs%d" % n], ns)
-            g.sync.dma_start(T.y[:, 256 * u:256 * v], T.ysb[:, 256 * u:256 * v]).then_inc(S["st%d" % n], 16)
-        for n in range(len(STORES)):
+        stores = 0
+        for n, (h, p) in enumerate((h, p) for h in halves for p in range(2)):
+            cs = sites[h][2 * p:2 * p + 2]
+            g.tensor.wait_ge(result(cs[0])[1], sum(2 * _nb(few(c) if onchip(c, core) else off_mask(c)) for c in cs))
+            o = result(cs[0])[0]
+            for b in range(4):
+                k, u = 512 * (4 * (n % 2) + b), 1024 * h + 256 * b
+                if n >= 2:
+                    g.tensor.wait_ge(S["cx%d" % (4 * (n - 2) + b)], 2)
+                g.tensor.matmul_mx(T.ps[:, k:k + 128], T.qsc[:, 128 * b:128 * b + 128], T.qsp[:, 128 * b:128 * b + 128],
+                                   T.rc[:, o:o + 128], T.rp[:, o:o + 128], True, True).then_inc(S["mx%d" % (4 * n + b)], 1)
+                q = g.scalar if b in BY_SCALAR[n] else g.vector
+                q.wait_ge(S["mx%d" % (4 * n + b)], 1)
+                for i in range(2):
+                    out, src = T.ysb[:, u + 2 * p + i:u + 256:4], T.ps[:, k + 64 * i:k + 64 * i + 64]
+                    x = g.scalar.activation(out, src, AF.Copy) if b in BY_SCALAR[n] else g.vector.tensor_copy(out, src)
+                    x.then_inc(S["cx%d" % (4 * n + b)], 1)
+            for u, v in STORES[n // 2] if p else []:
+                for b in range(u, v):
+                    g.sync.wait_ge(S["cx%d" % (4 * (n - 1) + b)], 2)
+                    g.sync.wait_ge(S["cx%d" % (4 * n + b)], 2)
+                u, v = 1024 * h + 256 * u, 1024 * h + 256 * v
+                g.sync.dma_start(T.y[:, u:v], T.ysb[:, u:v]).then_inc(S["st%d" % stores], 16)
+                stores += 1
+        for n in range(stores):
             g.sync.wait_ge(S["st%d" % n], 16)
         g.wait_ge(S.sent, sent[0])
         return
@@ -193,24 +230,35 @@ def rank_program(g, core, T, topo):
     g.vector.quantize_mx(T.qmc[:], T.qmp[:], T.sel[:]).then_inc(S.qs, 1)
     g.wait_ge(S.qs, 1)
     for w, m in ((1, few(core)), (0, off)):
-        send(w, [([r], m, 0, 128 * i, S.sm)], QM, QS, 128)
+        send(w, [([r], m, 0, QS, 128 * i, S.sm)], QM, 128)
     if r == root:
         for w, s, n in ((1, S.bfp, _nb(off_mask(root)) // 2), (0, S.bfc, _nb(on_mask(root)) // 2)):
             g.wait_ge(s, n)
-            send(w, [(bfar(i), off, 0, 128 * (i % 2), S.b)], F, B, 128)
+            send(w, [(bfar(i), off, 0, B, 128 * (i % 2), S.b)], F, 128)
+    if core == near[0]:
+        g.wait_ge(S.b, 2 * _nb(stay_mask(root)))
+        for w in (1, 0):
+            send(w, [(near[1:], stay_mask(core), 0, B, 0, S.b)], B, 256)
     h = 0 if r in g0 else 1
     n_ry = _nb(stay_mask(r)) // 2
     for w, s in ((1, S.ryp), (0, S.ryc)):
         g.wait_ge(s, n_ry)
-        send(w, [([sites[1 - h][i]], off, 0, place(r), landed(r))], Y, I, 128)
+        send(w, [([sites[1 - h][i]], off, 0, I, place(r), landed(r))], Y, 128)
+    for p in products:
+        if helper[p] == core:
+            for w, s in ((1, S.hlp), (0, S.hlc)):
+                g.wait_ge(s, _nb(rest(p)))
+                send(w, [(targets(p)[1], off, 0, R, result(p)[0], result(p)[1])], H, 64)
     if core not in sites[h]:
         g.wait_ge(S.sent, sent[0])
         return
 
-    if h == 0:
-        n_b = 2 * _nb(stay_mask(root) if r == root else off_mask(root))
-    else:
+    if h == 1:
         n_b = sum(2 * _nb(off_mask(c)) for q, c in enumerate(relay[root]) if core in bfar(q))
+    elif core in near:
+        n_b = 2 * _nb(stay_mask(root if core == near[0] else near[0]))
+    else:
+        n_b = 2 * _nb(off_mask(root))
     g.tensor.wait_ge(S.b, n_b)
     seq = [x for x in planes[h] if x != root] + planes[1 - h][::-1] + ([root] if h == 0 else [])
     for k, x in enumerate(seq):
@@ -222,31 +270,36 @@ def rank_program(g, core, T, topo):
             g.tensor.wait_ge(landed(x), sum(2 * _nb(m) for c, m, _ in direct(x) if c == core))
         else:
             g.tensor.wait_ge(landed(x), 2 * _nb(off_mask(relay[x][i])))
-        g.tensor.matmul_mx(T.ps[:, 512 * k:512 * k + 256], wc[:, o:o + 128], wp[:, o:o + 128],
-                           T.bc[:], T.bp[:], True, True).then_inc(S["mm%d" % k], 1)
-    for k in range(6):
-        g.scalar.wait_ge(S["mm%d" % k], 1)
-        out = T.relu[:, k:1280:5] if k < 5 else T.last[:]
-        g.scalar.activation(out, T.ps[:, 512 * k:512 * k + 256], AF.Relu).then_inc(S["re%d" % k], 1)
+        for u, a, n in [(k, 0, 256)] if k < 5 else [(5, 0, 128), (6, 128, 128)]:
+            g.tensor.matmul_mx(T.ps[:, 512 * u:512 * u + n], wc[:, o:o + 128], wp[:, o:o + 128],
+                               T.bc[:, a:a + n], T.bp[:, a:a + n], True, True).then_inc(S["mm%d" % u], 1)
+    for k in range(7):
+        if k not in VECTOR_TERMS:
+            g.scalar.wait_ge(S["mm%d" % k], 1)
+            out = T.relu[:, k:1280:5] if k < 5 else T.last[:, 128 * (k - 5):128 * (k - 4)]
+            g.scalar.activation(out, T.ps[:, 512 * k:512 * k + (256 if k < 5 else 128)], AF.Relu).then_inc(S["re%d" % k], 1)
     g.vector.memset(T.tile[:, 256:512], 0.0).then_inc(S.pad, 1)
     g.vector.memset(T.keep[:], 1.0).then_inc(S.pad, 1)
     g.vector.wait_ge(S.pad, 2)
     g.vector.memset(T.keep[:, 0:1280:5], 0.0).then_inc(S.msk, 1)
     g.vector.wait_ge(S.msk, 1)
+    for k in VECTOR_TERMS:
+        g.vector.wait_ge(S["mm%d" % k], 1)
+        g.vector.tensor_scalar(T.relu[:, k:1280:5], T.ps[:, 512 * k:512 * k + 256], 0.0, None,
+                               AluOpType.max).then_inc(S["re%d" % k], 1)
     for k in range(5):
         g.vector.wait_ge(S["re%d" % k], 1)
     g.vector.tensor_tensor_scan(T.acc[:], T.keep[:], T.relu[:], 0.0, AluOpType.mult, AluOpType.add).then_inc(S.sum, 1)
     g.vector.wait_ge(S.sum, 1)
-    g.vector.wait_ge(S.re5, 1)
     for t in range(4):
+        g.vector.wait_ge(S["re%d" % (5 + t // 2)], 1)
         g.vector.tensor_tensor(T.tile[:, t:256:4], T.acc[:, 320 * t + 4:320 * t + 320:5], T.last[:, 64 * t:64 * t + 64],
                                AluOpType.add).then_inc(S.tl, 1)
     g.vector.wait_ge(S.tl, 4)
     g.vector.quantize_mx(T.qtc[:], T.qtp[:], T.tile[:]).then_inc(S.qt, 1)
     g.wait_ge(S.qt, 1)
-    k = (4 * h + i) % len(T.cores)
-    to = T.cores[k:] + T.cores[:k]
-    for w in (0, 1):
-        send(w, [([c for c in to if onchip(c, core) == on], m, 0, 256 * h + 64 * i, S["res%d" % h])
-                 for on, m in ((False, off), (True, few(core)))], QT, R, 64)
+    out, _, own = targets(core)
+    o, s = result(core)
+    for w, hs in ((1, S.hlp), (0, S.hlc)):
+        send(w, [(out, off, 0, R, o, s), (own, few(core), 0, R, o, s), ([helper[core]], rest(core), 0, H, 0, hs)], QT, 64)
     g.wait_ge(S.sent, sent[0])

from concourse.bass import DstId, RemoteDMATransfer
from concourse.mybir import dt, AluOpType, ActivationFunctionType as AF

F8, U8 = "float8_e4m3fn_x4", "uint8"
SCRATCH = {
    "at": ("sbuf", [128, 2048], "bfloat16"),
    "bt": ("sbuf", [128, 2048], "bfloat16"),
    "qac": ("sbuf", [128, 512], F8), "qap": ("sbuf", [128, 512], U8),
    "qbc": ("sbuf", [128, 512], F8), "qbp": ("sbuf", [128, 512], U8),
    "qsc": ("sbuf", [128, 512], F8), "qsp": ("sbuf", [128, 512], U8),
    "rc": ("sbuf", [128, 512], F8), "rp": ("sbuf", [128, 512], U8),
    "ysb": ("sbuf", [128, 2048], "float32"),
    "sel": ("sbuf", [128, 512], "bfloat16"),
    "qmc": ("sbuf", [128, 128], F8), "qmp": ("sbuf", [128, 128], U8),
    "yc": ("sbuf", [128, 128], F8), "yp": ("sbuf", [128, 128], U8),
    "fc": ("sbuf", [128, 128], F8), "fp": ("sbuf", [128, 128], U8),
    "hc": ("sbuf", [128, 64], F8), "hp": ("sbuf", [128, 64], U8),
    "ic": ("sbuf", [128, 768], F8), "ip": ("sbuf", [128, 768], U8),
    "bc": ("sbuf", [128, 256], F8), "bp": ("sbuf", [128, 256], U8),
    "relu": ("sbuf", [128, 1280], "bfloat16"),
    "keep": ("sbuf", [128, 1280], "bfloat16"),
    "acc": ("sbuf", [128, 1280], "bfloat16"),
    "last": ("sbuf", [128, 256], "bfloat16"),
    "tile": ("sbuf", [128, 512], "bfloat16"),
    "qtc": ("sbuf", [128, 128], F8), "qtp": ("sbuf", [128, 128], U8),
    "ps": ("psum", [128, 4096], "float32"),
}
SEMAPHORES = (["la0", "la1", "lb0", "lb1", "ones", "onehot", "qa0", "qa1", "qb0", "qb1", "qs", "sent", "hlc", "hlp",
               "sm", "b", "bfp", "bfc", "ryp", "ryc", "pad", "qt", "msk", "sum", "tl"]
              + ["res%d" % k for k in range(4)] + ["st%d" % k for k in range(6)]
              + [p + "%d" % k for p in ("r", "re", "mm") for k in range(7)]
              + [p + "%d" % k for p in ("mx", "cx") for k in range(16)])
NCORES = 128
HOME = [[0, 0, 1, 2], [0, 1, 2, 0]]
FIRST = [3, 0]
HELPED = 2
STORES = [[(0, 2), (2, 4)], [(0, 1), (1, 2), (2, 3), (3, 4)]]
BY_SCALAR = [(1, 3), (1, 3), (1, 3), (1,)]
VECTOR_TERMS = (1, 3)


def _bits(mask):
    return [1 << k for k in range(mask.bit_length()) if (mask >> k) & 1]


def _nb(mask):
    return len(_bits(mask))


def _split(mask, n):
    e = _bits(mask)
    m = len(e) // n
    return [sum(e[k * m:(k + 1) * m]) for k in range(n)]


def rank_program(g, core, T, topo):
    S = T.sem
    root = T.cores[T.root]

    def onchip(c, d):
        return topo.chip(c) == topo.chip(d)

    def off_mask(c):
        return [topo.mask(c, d) for d in range(NCORES) if not onchip(c, d)][0]

    def on_mask(c):
        return [topo.mask(c, d) for d in range(NCORES) if d != c and onchip(c, d)][0]

    def stay_mask(c):
        return on_mask(c) & ~off_mask(c)

    def few(c):
        return _split(stay_mask(c), 2)[0]

    def rest(c):
        return _split(stay_mask(c), 2)[1]

    gates = [c for c in range(NCORES) if c not in T.cores and all(topo.may_write(c, r) for r in T.cores)]
    g0 = [root] + [r for r in T.cores if r != root and topo.same_plane(topo.chip(r), topo.chip(root))]
    g1 = [r for r in T.cores if r not in g0]
    planes = [g0, g1]
    sites = [[], []]
    for h in range(2):
        for i in range(4):
            r = planes[h][HOME[h][i]]
            have = [topo.die(s) for s in sites[h] if onchip(s, r)]
            d = 1 - have[0] if have else 1 - i % 2
            sites[h].append([c for c in gates if onchip(c, r) and c not in sites[h] and topo.die(c) == d][0])
    products = sites[0] + sites[1]
    relay = {}
    for r in T.cores:
        h = 0 if r in g0 else 1
        free = [c for c in gates if onchip(c, r) and c not in sites[h]]
        crowd = [len([s for s in sites[1 - h] if onchip(s, t)]) for t in sites[1 - h]]
        relay[r] = [s if onchip(s, r) else None for s in sites[h]]
        for i in sorted(range(4), key=lambda k: -crowd[k]):
            if relay[r][i] is None:
                fit = [c for c in free if (topo.die(c) != topo.die(r)) == (crowd[i] > 1)] or free
                relay[r][i] = fit[0]
                free.remove(fit[0])
    helper = {}
    for p in products:
        free = [c for c in gates if onchip(c, p) and c not in products and c not in helper.values()]
        helper[p] = ([c for c in free if topo.die(c) != topo.die(p)] or free)[0]
    order = g0 + g1
    near = [c for c in sites[0] if onchip(c, root)]

    def place(r):
        return 128 * order.index(r)

    def landed(r):
        return S["r%d" % order.index(r)]

    def direct(r):
        h = 0 if r in g0 else 1
        d = [(c, i) for i, c in enumerate(sites[h]) if not onchip(c, r)]
        return [(c, m, i) for (c, i), m in zip(d, _split(off_mask(r), 4 if len(d) == 3 else len(d)))]

    def bfar(q):
        return sites[1][2 * (q // 2):2 * (q // 2) + 2]

    def whose(p):
        h = 0 if p in sites[0] else 1
        return h, sites[h].index(p)

    def targets(p):
        k = FIRST[whose(p)[0]]
        to = T.cores[k:] + T.cores[:k]
        out = [c for c in to if not onchip(c, p)]
        return out[:-HELPED], out[-HELPED:], [c for c in to if onchip(c, p)]

    def result(p):
        h, i = whose(p)
        return 256 * h + 64 * i, S["res%d" % (2 * h + i // 2)]

    sent = [0]

    def dst(c):
        rid, pid, _ = topo.addr(c)
        return DstId(rid=rid, pnc=pid)

    def send(w, parts, src, n):
        def cut(k, a):
            return k[1][:, a:a + n] if w else k[0][:, a:a + n].bitcast(dt.uint8)
        parts = [p for p in parts if p[0]]
        g.remote_dma_fused([RemoteDMATransfer(dst_ids=[dst(c) for c in cs], dma_engine_mask=m, remote_sem=sem,
                                              srcs=[cut(src, a)], dsts=[cut(to, o)] * len(cs))
                            for cs, m, a, to, o, sem in parts], local_sem=S.sent)
        sent[0] += sum(_nb(p[1]) for p in parts)

    QA, QB, QT, QM, QS = (T.qac, T.qap), (T.qbc, T.qbp), (T.qtc, T.qtp), (T.qmc, T.qmp), (T.qsc, T.qsp)
    Y, F, I, B, R, H = (T.yc, T.yp), (T.fc, T.fp), (T.ic, T.ip), (T.bc, T.bp), (T.rc, T.rp), (T.hc, T.hp)

    if core in T.cores:
        loads = [(T.at, T.a, 0, 1024, S.la0), (T.at, T.a, 1024, 1024, S.la1)]
        if core == root:
            loads = [(T.bt, T.b, o, 512, S.lb1 if o >= 1024 else S.lb0) for o in (1024, 1536, 0, 512)] + loads
        for k, (d, s, o, n, sem) in enumerate(loads):
            (g.scalar if k % 2 else g.sync).dma_start(d[:, o:o + n], s[:, o:o + n]).then_inc(sem, 16)

        def quant(k, w, n, q, t, done):
            g.vector.wait_ge(w, n)
            g.vector.quantize_mx(q[0][:, k:k + 256], q[1][:, k:k + 256], t[:, 4 * k:4 * k + 1024]).then_inc(done, 1)

        if core == root:
            quant(256, S.lb1, 32, QB, T.bt, S.qb1)
            quant(0, S.lb0, 32, QB, T.bt, S.qb0)
        quant(0, S.la0, 16, QA, T.at, S.qa0)
        quant(256, S.la1, 16, QA, T.at, S.qa1)
        m, off, stay = on_mask(core), off_mask(core), stay_mask(core)
        if core == root:
            g.wait_ge(S.qb1, 1)
            for w, s, x in ((1, S.bfp, off), (0, S.bfc, m)):
                send(w, [([relay[root][j], relay[root][2 + j]], y, 256 + 128 * j, F, 0, s)
                         for j, y in enumerate(_split(x, 2))], QB, 128)
            g.wait_ge(S.qb0, 1)
            for w in (1, 0):
                send(w, [([c for c in sites[0] if not onchip(c, root)], off, 0, B, 0, S.b),
                         (near[:1], stay, 0, B, 0, S.b)], QB, 256)
        for p in range(2):
            g.wait_ge(S["qa%d" % p], 1)
            for w, s in ((1, S.ryp), (0, S.ryc)):
                send(w, [([relay[core][2 * p + k]], y, 128 * (2 * p + k), Y, 0, s) for k, y in enumerate(_split(stay, 2))],
                     QA, 128)
        for w in (1, 0):
            send(w, [([c], x, 128 * i, I, place(core), landed(core)) for c, x, i in direct(core)], QA, 128)

        me = T.cores.index(core)
        halves = sorted(range(2), key=lambda h: (me - FIRST[h]) % len(T.cores))
        g.tensor.wait_ge(S.sm, sum(_nb(few(c)) + _nb(off_mask(c)) for c in relay[core]))
        stores = 0
        for n, (h, p) in enumerate((h, p) for h in halves for p in range(2)):
            cs = sites[h][2 * p:2 * p + 2]
            g.tensor.wait_ge(result(cs[0])[1], sum(2 * _nb(few(c) if onchip(c, core) else off_mask(c)) for c in cs))
            o = result(cs[0])[0]
            for b in range(4):
                k, u = 512 * (4 * (n % 2) + b), 1024 * h + 256 * b
                if n >= 2:
                    g.tensor.wait_ge(S["cx%d" % (4 * (n - 2) + b)], 2)
                g.tensor.matmul_mx(T.ps[:, k:k + 128], T.qsc[:, 128 * b:128 * b + 128], T.qsp[:, 128 * b:128 * b + 128],
                                   T.rc[:, o:o + 128], T.rp[:, o:o + 128], True, True).then_inc(S["mx%d" % (4 * n + b)], 1)
                q = g.scalar if b in BY_SCALAR[n] else g.vector
                q.wait_ge(S["mx%d" % (4 * n + b)], 1)
                for i in range(2):
                    out, src = T.ysb[:, u + 2 * p + i:u + 256:4], T.ps[:, k + 64 * i:k + 64 * i + 64]
                    x = g.scalar.activation(out, src, AF.Copy) if b in BY_SCALAR[n] else g.vector.tensor_copy(out, src)
                    x.then_inc(S["cx%d" % (4 * n + b)], 1)
            for u, v in STORES[n // 2] if p else []:
                for b in range(u, v):
                    g.sync.wait_ge(S["cx%d" % (4 * (n - 1) + b)], 2)
                    g.sync.wait_ge(S["cx%d" % (4 * n + b)], 2)
                u, v = 1024 * h + 256 * u, 1024 * h + 256 * v
                g.sync.dma_start(T.y[:, u:v], T.ysb[:, u:v]).then_inc(S["st%d" % stores], 16)
                stores += 1
        for n in range(stores):
            g.sync.wait_ge(S["st%d" % n], 16)
        g.wait_ge(S.sent, sent[0])
        return

    mine = [r for r in T.cores if core in relay[r]]
    if not mine:
        return
    r = mine[0]
    i = relay[r].index(core)
    off = off_mask(core)
    g.vector.memset(T.sel[:], 1.0).then_inc(S.ones, 1)
    g.wait_ge(S.ones, 1)
    g.affine_select(T.sel[:], T.sel[:], [[-1, 512]], AluOpType.is_equal, 0.0, i, 4).then_inc(S.onehot, 1)
    g.vector.wait_ge(S.onehot, 1)
    g.vector.quantize_mx(T.qmc[:], T.qmp[:], T.sel[:]).then_inc(S.qs, 1)
    g.wait_ge(S.qs, 1)
    for w, m in ((1, few(core)), (0, off)):
        send(w, [([r], m, 0, QS, 128 * i, S.sm)], QM, 128)
    if r == root:
        for w, s, n in ((1, S.bfp, _nb(off_mask(root)) // 2), (0, S.bfc, _nb(on_mask(root)) // 2)):
            g.wait_ge(s, n)
            send(w, [(bfar(i), off, 0, B, 128 * (i % 2), S.b)], F, 128)
    if core == near[0]:
        g.wait_ge(S.b, 2 * _nb(stay_mask(root)))
        for w in (1, 0):
            send(w, [(near[1:], stay_mask(core), 0, B, 0, S.b)], B, 256)
    h = 0 if r in g0 else 1
    n_ry = _nb(stay_mask(r)) // 2
    for w, s in ((1, S.ryp), (0, S.ryc)):
        g.wait_ge(s, n_ry)
        send(w, [([sites[1 - h][i]], off, 0, I, place(r), landed(r))], Y, 128)
    for p in products:
        if helper[p] == core:
            for w, s in ((1, S.hlp), (0, S.hlc)):
                g.wait_ge(s, _nb(rest(p)))
                send(w, [(targets(p)[1], off, 0, R, result(p)[0], result(p)[1])], H, 64)
    if core not in sites[h]:
        g.wait_ge(S.sent, sent[0])
        return

    if h == 1:
        n_b = sum(2 * _nb(off_mask(c)) for q, c in enumerate(relay[root]) if core in bfar(q))
    elif core in near:
        n_b = 2 * _nb(stay_mask(root if core == near[0] else near[0]))
    else:
        n_b = 2 * _nb(off_mask(root))
    g.tensor.wait_ge(S.b, n_b)
    seq = [x for x in planes[h] if x != root] + planes[1 - h][::-1] + ([root] if h == 0 else [])
    for k, x in enumerate(seq):
        (wc, wp), o = (Y, 0) if x == r else (I, place(x))
        if x == r:
            g.tensor.wait_ge(S.ryp, n_ry)
            g.tensor.wait_ge(S.ryc, n_ry)
        elif x in planes[h]:
            g.tensor.wait_ge(landed(x), sum(2 * _nb(m) for c, m, _ in direct(x) if c == core))
        else:
            g.tensor.wait_ge(landed(x), 2 * _nb(off_mask(relay[x][i])))
        for u, a, n in [(k, 0, 256)] if k < 5 else [(5, 0, 128), (6, 128, 128)]:
            g.tensor.matmul_mx(T.ps[:, 512 * u:512 * u + n], wc[:, o:o + 128], wp[:, o:o + 128],
                               T.bc[:, a:a + n], T.bp[:, a:a + n], True, True).then_inc(S["mm%d" % u], 1)
    for k in range(7):
        if k not in VECTOR_TERMS:
            g.scalar.wait_ge(S["mm%d" % k], 1)
            out = T.relu[:, k:1280:5] if k < 5 else T.last[:, 128 * (k - 5):128 * (k - 4)]
            g.scalar.activation(out, T.ps[:, 512 * k:512 * k + (256 if k < 5 else 128)], AF.Relu).then_inc(S["re%d" % k], 1)
    g.vector.memset(T.tile[:, 256:512], 0.0).then_inc(S.pad, 1)
    g.vector.memset(T.keep[:], 1.0).then_inc(S.pad, 1)
    g.vector.wait_ge(S.pad, 2)
    g.vector.memset(T.keep[:, 0:1280:5], 0.0).then_inc(S.msk, 1)
    g.vector.wait_ge(S.msk, 1)
    for k in VECTOR_TERMS:
        g.vector.wait_ge(S["mm%d" % k], 1)
        g.vector.tensor_scalar(T.relu[:, k:1280:5], T.ps[:, 512 * k:512 * k + 256], 0.0, None,
                               AluOpType.max).then_inc(S["re%d" % k], 1)
    for k in range(5):
        g.vector.wait_ge(S["re%d" % k], 1)
    g.vector.tensor_tensor_scan(T.acc[:], T.keep[:], T.relu[:], 0.0, AluOpType.mult, AluOpType.add).then_inc(S.sum, 1)
    g.vector.wait_ge(S.sum, 1)
    for t in range(4):
        g.vector.wait_ge(S["re%d" % (5 + t // 2)], 1)
        g.vector.tensor_tensor(T.tile[:, t:256:4], T.acc[:, 320 * t + 4:320 * t + 320:5], T.last[:, 64 * t:64 * t + 64],
                               AluOpType.add).then_inc(S.tl, 1)
    g.vector.wait_ge(S.tl, 4)
    g.vector.quantize_mx(T.qtc[:], T.qtp[:], T.tile[:]).then_inc(S.qt, 1)
    g.wait_ge(S.qt, 1)
    out, _, own = targets(core)
    o, s = result(core)
    for w, hs in ((1, S.hlp), (0, S.hlc)):
        send(w, [(out, off, 0, R, o, s), (own, few(core), 0, R, o, s), ([helper[core]], rest(core), 0, H, 0, hs)], QT, 64)
    g.wait_ge(S.sent, sent[0])
